import numpy as np
import ml_dtypes


def mxq(x, axis, fmt="e4m3"):
    dtype, down = {"e4m3": (ml_dtypes.float8_e4m3fn, 7), "e5m2": (ml_dtypes.float8_e5m2, 14)}[fmt]
    v = np.moveaxis(np.asarray(x, np.float32).astype(ml_dtypes.bfloat16).astype(np.float64), axis, -1)
    blocks = v.reshape(v.shape[:-1] + (-1, 32))
    amax = np.abs(blocks).max(-1, keepdims=True)
    byte = np.maximum(np.where(amax > 0, np.frexp(amax)[1] - 1 + 127, 0) - down, 1)
    scale = np.exp2(byte - 127.0)
    codes = (blocks / scale).astype(np.float32).astype(dtype).astype(np.float64)
    return np.moveaxis((codes * scale).reshape(v.shape), -1, axis)


WIDE = False


def mx_kscale(k):
    if not WIDE:
        return np.ones(k)
    levels = np.array([10, -10, 5, -5, 0])
    if k % 512:
        return np.exp2(np.random.permutation(np.resize(levels, k // 32))).repeat(32)
    a = np.empty((k // 512, 16))
    for p in range(k // 512):
        a[p, :8] = np.random.permutation(np.resize(levels, 8))
        for g in range(8):
            far = levels[np.abs(levels - a[p, g]) >= 10]
            a[p, g + 8] = far[np.random.randint(len(far))]
    return np.exp2(a.ravel()).repeat(32)


def f64(x):
    return np.asarray(x).astype(np.float64)


def striped(idx):
    return np.tile(np.asarray(idx).reshape(-1, 16).T, (8, 1)).astype(np.uint16)


def unstriped(offs):
    return offs[:16].T.reshape(-1).astype(np.int64)


E2M1 = np.array([0.0, 0.5, 1.0, 1.5, 2.0, 3.0, 4.0, 6.0, -0.0, -0.5, -1.0, -1.5, -2.0, -3.0, -4.0, -6.0])


def pack_weight(w, fmt):
    k, n = w.shape
    w = f64(np.asarray(w, np.float32).astype(ml_dtypes.bfloat16)).reshape(k // 32, 32, n)
    amax = np.abs(w).max(1)
    if fmt == "e4m3":
        byte = np.frexp(amax)[1] - 1 + 127 - 7
    else:
        mant, ex = np.frexp(amax / 6.0)
        byte = np.where(mant > 0.5, ex, ex - 1) + 127
    byte = np.clip(np.where(amax > 0, byte, 1), 1, 254)
    scaled = (w * np.exp2(127.0 - byte)[:, None, :]).reshape(k, n).astype(np.float32)
    by_word = np.ascontiguousarray(scaled.reshape(k // 512, 128, 4, n).transpose(0, 1, 3, 2))
    if fmt == "e4m3":
        words = by_word.astype(ml_dtypes.float8_e4m3fn).view(np.uint8)
    else:
        c = by_word.astype(ml_dtypes.float4_e2m1fn).view(np.uint8) & 0xF
        words = (c[..., 0::2] | (c[..., 1::2] << 4)).reshape(k // 512, 128, 2 * n)
    return np.ascontiguousarray(words), np.ascontiguousarray(byte.astype(np.uint8).reshape(k // 512, 16, n))


def unpack_weight(words, scales, fmt):
    g, _, n = scales.shape
    words = np.ascontiguousarray(words).reshape(g, 128, n, -1)
    if fmt == "e4m3":
        vals = words.view(ml_dtypes.float8_e4m3fn).astype(np.float64)
    else:
        nib = np.empty((g, 128, n, 4), np.uint8)
        nib[..., 0::2] = words & 0xF
        nib[..., 1::2] = words >> 4
        vals = E2M1[nib]
    vals = vals * np.repeat(np.exp2(scales.astype(np.float64) - 127.0), 8, axis=1)[..., None]
    return vals.transpose(0, 1, 3, 2).reshape(g * 512, n)


K, R, F, T, J, M = 512, 128, 512, 2048, 512, 256


def setup_inputs():
    n = np.random.standard_normal
    idx = np.random.permutation(T)[:J]
    idx2 = np.random.permutation(J)[:M]
    idx3 = np.random.permutation(J)[:M]
    idx4 = np.random.permutation(J)[:M]
    fk = mx_kscale(K)
    ff = mx_kscale(F)
    tabp = pack_weight(n((K, T)) / fk[:, None], "e2m1")
    return {
        "tab_words": tabp[0],
        "tab_scales": tabp[1],
        "w1": (n((K, R)) * 1 / np.sqrt(K) * fk[:, None]).astype(np.float32),
        "temper": (np.random.uniform(0.6, 2.0, (R, 1))).astype(np.float32),
        "wo": (n((F, R)) * 1 / np.sqrt(F) * ff[:, None]).astype(np.float32),
        "dy": (n((F, M)) / ff[:, None]).astype(np.float32),
        "old": (0.5 * n((R, J))).astype(np.float32),
        "offs": striped(idx),
        "offs2": striped(idx2),
        "offs3": striped(idx3),
        "offs4": striped(idx4),
    }


def reference(tab_words, tab_scales, w1, temper, wo, dy, old, offs, offs2, offs3, offs4):
    idx = unstriped(offs)
    idx2 = unstriped(offs2)
    idx3 = unstriped(offs3)
    idx4 = unstriped(offs4)
    tabu = unpack_weight(tab_words, tab_scales, "e2m1")
    w1q = mxq(f64(w1), 0, "e4m3")
    tabidxg = tabu[:, idx]
    a = w1q.T @ tabidxg
    e1s = np.exp(a * f64(temper) * (-1.0))
    s = e1s[:, idx2] + e1s[:, idx3] + e1s[:, idx4]
    woq = mxq(f64(wo), 0, "e4m3")
    dyq = mxq(f64(dy), 0, "e4m3")
    c0 = woq.T @ dyq
    ds = c0 * (-1.0) / f64(temper) / s
    s1 = np.zeros((R, J))
    s1[:, idx2] = ds
    s2 = np.zeros((R, J))
    s2[:, idx3] = ds
    s3 = np.zeros((R, J))
    s3[:, idx4] = ds
    de1s = s1 + s2 + s3
    da = de1s * e1s * (-1.0) * f64(temper)
    y = da + f64(old)
    return y

@@ -1,0 +1,149 @@
+from contextlib import ExitStack
+
+import concourse.mybir as mybir
+
+K, R, F, T, J, M = 512, 128, 512, 2048, 512, 256
+FLOPS = 2 * R * K * J + 2 * R * F * M
+
+F32 = mybir.dt.float32
+BF16 = mybir.dt.bfloat16
+I32 = mybir.dt.int32
+U32 = mybir.dt.uint32
+U16 = mybir.dt.uint16
+U8 = mybir.dt.uint8
+FP8X4 = mybir.dt.float8_e4m3fn_x4
+FP4X4 = mybir.dt.float4_e2m1fn_x4
+ACT = mybir.ActivationFunctionType
+ALU = mybir.AluOpType
+
+P = 128
+PACK = 4
+
+
+def tile_attend_csoftleast_kernel(tc, tab_words, tab_scales, w1, temper, wo, dy, old, offs, offs2, offs3, offs4, out):
+    nc = tc.nc
+    with ExitStack() as ctx:
+        keep = ctx.enter_context(tc.tile_pool(name="keep", bufs=1))
+        psum = ctx.enter_context(tc.psum_pool(name="psum", bufs=1))
+
+        slots = keep.tile([P, J // 16], U16)
+        picks = [keep.tile([P, M // 16], U16, name="picks%d" % i) for i in range(3)]
+        words = keep.tile([P, T], U16, align_bytes=64)
+        plane = keep.tile([P, T], U8, align_bytes=64)
+        w1_raw = keep.tile([P, PACK * R], F32)
+        placed = [keep.tile([P, J], F32, name="placed%d" % i) for i in range(3)]
+        ident = keep.tile([P, P], F32)
+
+        plane32 = plane[:].bitcast(I32)
+        nc.vector.memset(plane32, 0)
+        temper_col = keep.tile([P, 1], F32)
+        nc.gpsimd.dma_start(out=temper_col[:], in_=temper)
+        nc.sync.dma_start(slots[:], offs)
+        nc.sync.dma_start(picks[0][:], offs2)
+        nc.sync.dma_start(out=words[:].bitcast(I32), in_=tab_words[0].bitcast(I32))
+        nc.sync.dma_start(out=w1_raw[:], in_=w1.rearrange("(p j) w -> p (j w)", j=PACK))
+        nc.sync.dma_start(picks[1][:], offs3)
+        nc.sync.dma_start(picks[2][:], offs4)
+        scales32 = tab_scales[0].bitcast(I32)
+        for r in range(4):
+            nc.sync.dma_start(out=plane32[r:P:32, :], in_=scales32[r:16:4, :])
+
+        zeros = keep.tile([P, P], F32, tag="later")
+        nc.vector.memset(zeros[:], 0.0)
+        nc.gpsimd.affine_select(out=ident[:], in_=zeros[:], compare_op=ALU.not_equal, fill=1.0, base=0,
+                                pattern=[[-1, P]], channel_multiplier=1)
+        for tile in placed:
+            nc.vector.memset(tile[:], 0.0)
+
+        later = keep.tile([P, PACK * M + PACK * R + J], F32, tag="later")
+        dy_raw = later[:, : PACK * M]
+        wo_raw = later[:, PACK * M : PACK * (M + R)]
+        old_sb = later[:, PACK * (M + R) : PACK * (M + R) + J]
+        nc.sync.dma_start(out=dy_raw, in_=dy.rearrange("(p j) w -> p (j w)", j=PACK))
+        nc.sync.dma_start(out=wo_raw, in_=wo.rearrange("(p j) w -> p (j w)", j=PACK))
+        nc.sync.dma_start(out=old_sb, in_=old)
+
+        def interleave(copy, name, raw, width):
+            grouped = keep.tile([P, width, PACK], BF16, align_bytes=64, name=name + "_grouped")
+            copy(out=grouped[:], in_=raw.rearrange("p (j w) -> p w j", j=PACK))
+            return grouped
+
+        def quantize(name, grouped, width):
+            codes = keep.tile([P, width], U32, align_bytes=64, name=name + "_codes")
+            scales = keep.tile([P, width], U8, align_bytes=64, name=name + "_scales")
+            nc.vector.quantize_mx(out=codes[:].bitcast(FP8X4), scales=scales[:], in_=grouped[:].rearrange("p w j -> p (w j)"))
+            return codes, scales
+
+        w1_grouped = interleave(nc.scalar.copy, "w1", w1_raw[:], R)
+        minus_temper = keep.tile([P, 1], F32)
+        nc.scalar.activation(out=minus_temper[:], in_=temper_col[:], func=ACT.Copy, scale=-1.0)
+
+        HALF = J // 2
+        got_words = [keep.tile([P, HALF], U16, align_bytes=64, name="got_words%d" % h) for h in range(2)]
+        got_scales = [keep.tile([P, HALF], U8, align_bytes=64, name="got_scales%d" % h) for h in range(2)]
+        lists = [slots[:, h * HALF // 16 : (h + 1) * HALF // 16] for h in range(2)]
+        for h in range(2):
+            nc.vector.tensor_copy(got_words[h][:], words[:].indirect(lists[h]))
+        nc.vector.tensor_copy(got_scales[0][:], plane[:].indirect(lists[0]))
+        w1_codes, w1_scales = quantize("w1", w1_grouped, R)
+        nc.vector.tensor_copy(got_scales[1][:], plane[:].indirect(lists[1]))
+
+        e1s = keep.tile([P, J], F32)
+        for h in range(2):
+            a = psum.tile([P, HALF], F32, name="a%d" % h, tag="half%d" % h)
+            nc.tensor.matmul_mx(out=a[:], lhsT=w1_codes[:].bitcast(FP8X4), lhsT_scale=w1_scales[:],
+                                rhs=got_words[h][:].bitcast(FP4X4), rhs_scale=got_scales[h][:], start=True, stop=True)
+            nc.scalar.activation(out=e1s[:, h * HALF : (h + 1) * HALF], in_=a[:], func=ACT.Exp, scale=minus_temper[:])
+
+        dy_grouped = interleave(nc.vector.tensor_copy, "dy", dy_raw, M)
+        wo_grouped = interleave(nc.scalar.copy, "wo", wo_raw, R)
+        dy_codes, dy_scales = quantize("dy", dy_grouped, M)
+
+        PART = M // 2
+        got = [keep.tile([P, M], F32, name="got%d" % i) for i in range(3)]
+        pair = keep.tile([P, M], F32)
+        s = keep.tile([P, M], F32)
+        root = keep.tile([P, M], F32)
+        inv = keep.tile([P, M], F32)
+        ratio = keep.tile([P, M], F32)
+        for h in range(2):
+            cols = slice(h * PART, (h + 1) * PART)
+            lcols = slice(h * PART // 16, (h + 1) * PART // 16)
+            for i in range(3):
+                nc.vector.tensor_copy(got[i][:, cols], e1s[:].indirect(picks[i][:, lcols]))
+            nc.vector.tensor_tensor(pair[:, cols], got[0][:, cols], got[1][:, cols], ALU.add)
+            nc.vector.tensor_tensor(s[:, cols], pair[:, cols], got[2][:, cols], ALU.add)
+            if h == 0:
+                wo_codes, wo_scales = quantize("wo", wo_grouped, R)
+                c0 = psum.tile([P, M], F32)
+                nc.tensor.matmul_mx(out=c0[:], lhsT=wo_codes[:].bitcast(FP8X4), lhsT_scale=wo_scales[:],
+                                    rhs=dy_codes[:].bitcast(FP8X4), rhs_scale=dy_scales[:], start=True, stop=True)
+            nc.scalar.activation(out=root[:, cols], in_=s[:, cols], func=ACT.Abs_reciprocal_sqrt)
+            nc.scalar.activation(out=inv[:, cols], in_=root[:, cols], func=ACT.Square)
+
+        for h in range(2):
+            cols = slice(h * PART, (h + 1) * PART)
+            lcols = slice(h * PART // 16, (h + 1) * PART // 16)
+            nc.vector.tensor_tensor(ratio[:, cols], c0[:, cols], inv[:, cols], ALU.mult)
+            nc.vector.tensor_tensor(placed[0][:].indirect(picks[0][:, lcols]), ratio[:, cols], got[0][:, cols], ALU.mult)
+        for i in (1, 2):
+            nc.vector.tensor_tensor(placed[i][:].indirect(picks[i][:]), ratio[:], got[i][:], ALU.mult)
+
+        turned = keep.tile([P, J], F32)
+        back = [psum.tile([P, HALF], F32, name="back%d" % h, tag="half%d" % h) for h in range(2)]
+        sums = [psum.tile([P, P], F32, name="sums%d" % b) for b in range(J // P)]
+        terms = (old_sb, placed[0][:], placed[1][:])
+        for n, term in enumerate(terms):
+            for b in range(J // P):
+                nc.tensor.matmul(out=sums[b][:], lhsT=term[:, b * P : (b + 1) * P], rhs=ident[:],
+                                 start=(n == 0), stop=(n == len(terms) - 1), is_transpose=True)
+        for b in range(J // P):
+            nc.scalar.copy(out=turned[:, b * P : (b + 1) * P], in_=sums[b][:])
+        for b in range(J // P):
+            nc.tensor.transpose(back[b // 2][:, b % 2 * P : (b % 2 + 1) * P], turned[:, b * P : (b + 1) * P], ident[:])
+
+        result = [keep.tile([P, HALF], F32, name="result%d" % h) for h in range(2)]
+        for h, queue in enumerate((nc.sync, nc.scalar)):
+            cols = slice(h * HALF, (h + 1) * HALF)
+            nc.vector.tensor_tensor(result[h][:], back[h][:], placed[2][:, cols], ALU.add)
+            queue.dma_start(out=out[:, cols], in_=result[h][:])

@@ -36,35 +36,37 @@ def tile_attend_csoftleast_kernel(tc, tab_words, tab_scales, w1, temper, wo, dy,
 
         plane32 = plane[:].bitcast(I32)
         nc.vector.memset(plane32, 0)
-        temper_col = keep.tile([P, 1], F32)
-        nc.gpsimd.dma_start(out=temper_col[:], in_=temper)
+        temper_col = keep.tile([P, 1], F32, tag="after_temper")
+        nc.scalar.dma_start(out=temper_col[:], in_=temper)
         nc.sync.dma_start(slots[:], offs)
-        nc.sync.dma_start(picks[0][:], offs2)
+        for tile, src in zip(picks, (offs2, offs3, offs4)):
+            nc.sync.dma_start(tile[:], src)
         nc.sync.dma_start(out=words[:].bitcast(I32), in_=tab_words[0].bitcast(I32))
         nc.sync.dma_start(out=w1_raw[:], in_=w1.rearrange("(p j) w -> p (j w)", j=PACK))
-        nc.sync.dma_start(picks[1][:], offs3)
-        nc.sync.dma_start(picks[2][:], offs4)
         scales32 = tab_scales[0].bitcast(I32)
         for r in range(4):
             nc.sync.dma_start(out=plane32[r:P:32, :], in_=scales32[r:16:4, :])
 
-        zeros = keep.tile([P, P], F32, tag="later")
+        zeros = keep.tile([P, P], F32, tag="after_zeros")
         nc.vector.memset(zeros[:], 0.0)
         nc.gpsimd.affine_select(out=ident[:], in_=zeros[:], compare_op=ALU.not_equal, fill=1.0, base=0,
                                 pattern=[[-1, P]], channel_multiplier=1)
         for tile in placed:
             nc.vector.memset(tile[:], 0.0)
 
-        later = keep.tile([P, PACK * M + PACK * R + J], F32, tag="later")
+        minus_temper = keep.tile([P, 1], F32)
+        nc.scalar.activation(out=minus_temper[:], in_=temper_col[:], func=ACT.Copy, scale=-1.0)
+
+        wo_raw = keep.tile([P, PACK * R], F32, tag="after_zeros")
+        later = keep.tile([P, PACK * M + J], F32, tag="after_temper")
         dy_raw = later[:, : PACK * M]
-        wo_raw = later[:, PACK * M : PACK * (M + R)]
-        old_sb = later[:, PACK * (M + R) : PACK * (M + R) + J]
+        old_sb = later[:, PACK * M :]
+        nc.sync.dma_start(out=wo_raw[:], in_=wo.rearrange("(p j) w -> p (j w)", j=PACK))
         nc.sync.dma_start(out=dy_raw, in_=dy.rearrange("(p j) w -> p (j w)", j=PACK))
-        nc.sync.dma_start(out=wo_raw, in_=wo.rearrange("(p j) w -> p (j w)", j=PACK))
         nc.sync.dma_start(out=old_sb, in_=old)
 
         def interleave(copy, name, raw, width):
-            grouped = keep.tile([P, width, PACK], BF16, align_bytes=64, name=name + "_grouped")
+            grouped = keep.tile([P, width, PACK], BF16, align_bytes=64, name=name + "_grouped", tag=name + "_grouped")
             copy(out=grouped[:], in_=raw.rearrange("p (j w) -> p w j", j=PACK))
             return grouped
 
@@ -75,8 +77,8 @@ def tile_attend_csoftleast_kernel(tc, tab_words, tab_scales, w1, temper, wo, dy,
             return codes, scales
 
         w1_grouped = interleave(nc.scalar.copy, "w1", w1_raw[:], R)
-        minus_temper = keep.tile([P, 1], F32)
-        nc.scalar.activation(out=minus_temper[:], in_=temper_col[:], func=ACT.Copy, scale=-1.0)
+
+        wo_grouped = interleave(nc.scalar.copy, "wo", wo_raw[:], R)
 
         HALF = J // 2
         got_words = [keep.tile([P, HALF], U16, align_bytes=64, name="got_words%d" % h) for h in range(2)]
@@ -88,46 +90,45 @@ def tile_attend_csoftleast_kernel(tc, tab_words, tab_scales, w1, temper, wo, dy,
         w1_codes, w1_scales = quantize("w1", w1_grouped, R)
         nc.vector.tensor_copy(got_scales[1][:], plane[:].indirect(lists[1]))
 
-        e1s = keep.tile([P, J], F32)
+        e1s = keep.tile([P, J], F32, tag="after_zeros")
         for h in range(2):
             a = psum.tile([P, HALF], F32, name="a%d" % h, tag="half%d" % h)
             nc.tensor.matmul_mx(out=a[:], lhsT=w1_codes[:].bitcast(FP8X4), lhsT_scale=w1_scales[:],
                                 rhs=got_words[h][:].bitcast(FP4X4), rhs_scale=got_scales[h][:], start=True, stop=True)
             nc.scalar.activation(out=e1s[:, h * HALF : (h + 1) * HALF], in_=a[:], func=ACT.Exp, scale=minus_temper[:])
 
-        dy_grouped = interleave(nc.vector.tensor_copy, "dy", dy_raw, M)
-        wo_grouped = interleave(nc.scalar.copy, "wo", wo_raw, R)
-        dy_codes, dy_scales = quantize("dy", dy_grouped, M)
+        warm = keep.tile([P, 1], F32)
+        nc.scalar.activation(out=warm[:], in_=a[:, 0:1], func=ACT.Abs_reciprocal_sqrt, scale=0.0, bias=1.0)
 
         PART = M // 2
-        got = [keep.tile([P, M], F32, name="got%d" % i) for i in range(3)]
+        first, second = slice(0, PART), slice(PART, M)
+        dy_grouped = interleave(nc.vector.tensor_copy, "dy", dy_raw, M)
+        wo_codes, wo_scales = quantize("wo", wo_grouped, R)
+        dy_codes, dy_scales = quantize("dy", dy_grouped, M)
+        c0 = psum.tile([P, M], F32)
+        nc.tensor.matmul_mx(out=c0[:], lhsT=wo_codes[:].bitcast(FP8X4), lhsT_scale=wo_scales[:],
+                            rhs=dy_codes[:].bitcast(FP8X4), rhs_scale=dy_scales[:], start=True, stop=True)
+
+        picked = keep.tile([P, 3 * M], F32, align_bytes=64, tag="dy_grouped")
+        got = [picked[:, i * M : (i + 1) * M] for i in range(3)]
+        weighted = [keep.tile([P, M], F32, name="weighted%d" % i) for i in range(3)]
         pair = keep.tile([P, M], F32)
         s = keep.tile([P, M], F32)
         root = keep.tile([P, M], F32)
         inv = keep.tile([P, M], F32)
-        ratio = keep.tile([P, M], F32)
-        for h in range(2):
-            cols = slice(h * PART, (h + 1) * PART)
-            lcols = slice(h * PART // 16, (h + 1) * PART // 16)
-            for i in range(3):
-                nc.vector.tensor_copy(got[i][:, cols], e1s[:].indirect(picks[i][:, lcols]))
-            nc.vector.tensor_tensor(pair[:, cols], got[0][:, cols], got[1][:, cols], ALU.add)
+        for i in range(3):
+            nc.vector.tensor_copy(got[i], e1s[:].indirect(picks[i][:]))
+        nc.vector.tensor_tensor(pair[:], got[0], got[1], ALU.add)
+        nc.vector.tensor_tensor(weighted[0][:], c0[:], got[0], ALU.mult)
+        for cols in (first, second):
             nc.vector.tensor_tensor(s[:, cols], pair[:, cols], got[2][:, cols], ALU.add)
-            if h == 0:
-                wo_codes, wo_scales = quantize("wo", wo_grouped, R)
-                c0 = psum.tile([P, M], F32)
-                nc.tensor.matmul_mx(out=c0[:], lhsT=wo_codes[:].bitcast(FP8X4), lhsT_scale=wo_scales[:],
-                                    rhs=dy_codes[:].bitcast(FP8X4), rhs_scale=dy_scales[:], start=True, stop=True)
             nc.scalar.activation(out=root[:, cols], in_=s[:, cols], func=ACT.Abs_reciprocal_sqrt)
+        for cols in (first, second):
             nc.scalar.activation(out=inv[:, cols], in_=root[:, cols], func=ACT.Square)
-
-        for h in range(2):
-            cols = slice(h * PART, (h + 1) * PART)
-            lcols = slice(h * PART // 16, (h + 1) * PART // 16)
-            nc.vector.tensor_tensor(ratio[:, cols], c0[:, cols], inv[:, cols], ALU.mult)
-            nc.vector.tensor_tensor(placed[0][:].indirect(picks[0][:, lcols]), ratio[:, cols], got[0][:, cols], ALU.mult)
         for i in (1, 2):
-            nc.vector.tensor_tensor(placed[i][:].indirect(picks[i][:]), ratio[:], got[i][:], ALU.mult)
+            nc.vector.tensor_tensor(weighted[i][:], c0[:], got[i], ALU.mult)
+        for i in range(3):
+            nc.vector.tensor_tensor(placed[i][:].indirect(picks[i][:]), weighted[i][:], inv[:], ALU.mult)
 
         turned = keep.tile([P, J], F32)
         back = [psum.tile([P, HALF], F32, name="back%d" % h, tag="half%d" % h) for h in range(2)]

@@ -36,13 +36,13 @@ def tile_attend_csoftleast_kernel(tc, tab_words, tab_scales, w1, temper, wo, dy,
 
         plane32 = plane[:].bitcast(I32)
         nc.vector.memset(plane32, 0)
-        temper_col = keep.tile([P, 1], F32, tag="after_temper")
-        nc.scalar.dma_start(out=temper_col[:], in_=temper)
+        temper_col = keep.tile([P, 1], F32)
         nc.sync.dma_start(slots[:], offs)
+        nc.scalar.dma_start(out=w1_raw[:], in_=w1.rearrange("(p j) w -> p (j w)", j=PACK))
+        nc.scalar.dma_start(out=temper_col[:], in_=temper)
         for tile, src in zip(picks, (offs2, offs3, offs4)):
             nc.sync.dma_start(tile[:], src)
         nc.sync.dma_start(out=words[:].bitcast(I32), in_=tab_words[0].bitcast(I32))
-        nc.sync.dma_start(out=w1_raw[:], in_=w1.rearrange("(p j) w -> p (j w)", j=PACK))
         scales32 = tab_scales[0].bitcast(I32)
         for r in range(4):
             nc.sync.dma_start(out=plane32[r:P:32, :], in_=scales32[r:16:4, :])
@@ -54,14 +54,11 @@ def tile_attend_csoftleast_kernel(tc, tab_words, tab_scales, w1, temper, wo, dy,
         for tile in placed:
             nc.vector.memset(tile[:], 0.0)
 
-        minus_temper = keep.tile([P, 1], F32)
-        nc.scalar.activation(out=minus_temper[:], in_=temper_col[:], func=ACT.Copy, scale=-1.0)
-
-        wo_raw = keep.tile([P, PACK * R], F32, tag="after_zeros")
-        later = keep.tile([P, PACK * M + J], F32, tag="after_temper")
-        dy_raw = later[:, : PACK * M]
-        old_sb = later[:, PACK * M :]
-        nc.sync.dma_start(out=wo_raw[:], in_=wo.rearrange("(p j) w -> p (j w)", j=PACK))
+        later = keep.tile([P, PACK * (R + M) + J], F32, tag="after_zeros")
+        wo_raw = later[:, : PACK * R]
+        dy_raw = later[:, PACK * R : PACK * (R + M)]
+        old_sb = later[:, PACK * (R + M) :]
+        nc.sync.dma_start(out=wo_raw, in_=wo.rearrange("(p j) w -> p (j w)", j=PACK))
         nc.sync.dma_start(out=dy_raw, in_=dy.rearrange("(p j) w -> p (j w)", j=PACK))
         nc.sync.dma_start(out=old_sb, in_=old)
 
@@ -78,24 +75,26 @@ def tile_attend_csoftleast_kernel(tc, tab_words, tab_scales, w1, temper, wo, dy,
 
         w1_grouped = interleave(nc.scalar.copy, "w1", w1_raw[:], R)
 
-        wo_grouped = interleave(nc.scalar.copy, "wo", wo_raw[:], R)
+        wo_grouped = interleave(nc.scalar.copy, "wo", wo_raw, R)
+        minus_temper = wo_raw[:, 0:1]
+        nc.scalar.activation(out=minus_temper, in_=temper_col[:], func=ACT.Copy, scale=-1.0)
 
         HALF = J // 2
         got_words = [keep.tile([P, HALF], U16, align_bytes=64, name="got_words%d" % h) for h in range(2)]
         got_scales = [keep.tile([P, HALF], U8, align_bytes=64, name="got_scales%d" % h) for h in range(2)]
         lists = [slots[:, h * HALF // 16 : (h + 1) * HALF // 16] for h in range(2)]
+        w1_codes, w1_scales = quantize("w1", w1_grouped, R)
         for h in range(2):
             nc.vector.tensor_copy(got_words[h][:], words[:].indirect(lists[h]))
-        nc.vector.tensor_copy(got_scales[0][:], plane[:].indirect(lists[0]))
-        w1_codes, w1_scales = quantize("w1", w1_grouped, R)
-        nc.vector.tensor_copy(got_scales[1][:], plane[:].indirect(lists[1]))
-
-        e1s = keep.tile([P, J], F32, tag="after_zeros")
         for h in range(2):
-            a = psum.tile([P, HALF], F32, name="a%d" % h, tag="half%d" % h)
+            nc.vector.tensor_copy(got_scales[h][:], plane[:].indirect(lists[h]))
+
+        e1s = keep.tile([P, J], F32)
+        for h, lo, hi, bank in ((0, 0, HALF, "half0"), (1, 0, P, "third"), (1, P, HALF, "half1")):
+            a = psum.tile([P, hi - lo], F32, name="a_" + bank, tag=bank)
             nc.tensor.matmul_mx(out=a[:], lhsT=w1_codes[:].bitcast(FP8X4), lhsT_scale=w1_scales[:],
-                                rhs=got_words[h][:].bitcast(FP4X4), rhs_scale=got_scales[h][:], start=True, stop=True)
-            nc.scalar.activation(out=e1s[:, h * HALF : (h + 1) * HALF], in_=a[:], func=ACT.Exp, scale=minus_temper[:])
+                                rhs=got_words[h][:, lo:hi].bitcast(FP4X4), rhs_scale=got_scales[h][:, lo:hi], start=True, stop=True)
+            nc.scalar.activation(out=e1s[:, h * HALF + lo : h * HALF + hi], in_=a[:], func=ACT.Exp, scale=minus_temper)
 
         warm = keep.tile([P, 1], F32)
         nc.scalar.activation(out=warm[:], in_=a[:, 0:1], func=ACT.Abs_reciprocal_sqrt, scale=0.0, bias=1.0)
@@ -111,24 +110,25 @@ def tile_attend_csoftleast_kernel(tc, tab_words, tab_scales, w1, temper, wo, dy,
 
         picked = keep.tile([P, 3 * M], F32, align_bytes=64, tag="dy_grouped")
         got = [picked[:, i * M : (i + 1) * M] for i in range(3)]
-        weighted = [keep.tile([P, M], F32, name="weighted%d" % i) for i in range(3)]
-        pair = keep.tile([P, M], F32)
+        products = keep.tile([P, 3 * M], F32)
+        weighted = [products[:, i * M : (i + 1) * M] for i in range(3)]
+        pair = (products[:, 2 * M : 2 * M + PART], products[:, M - PART // 2 : M + PART // 2])
         s = keep.tile([P, M], F32)
         root = keep.tile([P, M], F32)
         inv = keep.tile([P, M], F32)
         for i in range(3):
             nc.vector.tensor_copy(got[i], e1s[:].indirect(picks[i][:]))
-        nc.vector.tensor_tensor(pair[:], got[0], got[1], ALU.add)
-        nc.vector.tensor_tensor(weighted[0][:], c0[:], got[0], ALU.mult)
-        for cols in (first, second):
-            nc.vector.tensor_tensor(s[:, cols], pair[:, cols], got[2][:, cols], ALU.add)
+        for h, cols in enumerate((first, second)):
+            nc.vector.tensor_tensor(pair[h], got[0][:, cols], got[1][:, cols], ALU.add)
+        for h, cols in enumerate((first, second)):
+            nc.vector.tensor_tensor(s[:, cols], pair[h], got[2][:, cols], ALU.add)
             nc.scalar.activation(out=root[:, cols], in_=s[:, cols], func=ACT.Abs_reciprocal_sqrt)
         for cols in (first, second):
             nc.scalar.activation(out=inv[:, cols], in_=root[:, cols], func=ACT.Square)
-        for i in (1, 2):
-            nc.vector.tensor_tensor(weighted[i][:], c0[:], got[i], ALU.mult)
         for i in range(3):
-            nc.vector.tensor_tensor(placed[i][:].indirect(picks[i][:]), weighted[i][:], inv[:], ALU.mult)
+            nc.vector.tensor_tensor(weighted[i], c0[:], got[i], ALU.mult)
+        for i in range(3):
+            nc.vector.tensor_tensor(placed[i][:].indirect(picks[i][:]), weighted[i], inv[:], ALU.mult)
 
         turned = keep.tile([P, J], F32)
         back = [psum.tile([P, HALF], F32, name="back%d" % h, tag="half%d" % h) for h in range(2)]

@@ -64,7 +64,7 @@ def tile_attend_csoftleast_kernel(tc, tab_words, tab_scales, w1, temper, wo, dy,
 
         def interleave(copy, name, raw, width):
             grouped = keep.tile([P, width, PACK], BF16, align_bytes=64, name=name + "_grouped", tag=name + "_grouped")
-            copy(out=grouped[:], in_=raw.rearrange("p (j w) -> p w j", j=PACK))
+            copy(out=grouped[:].rearrange("p (c i) j -> p c j i", i=PACK), in_=raw.rearrange("p (j c i) -> p c j i", j=PACK, i=PACK))
             return grouped
 
         def quantize(name, grouped, width):

from contextlib import ExitStack

import concourse.mybir as mybir

K, R, F, T, J, M = 512, 128, 512, 2048, 512, 256
FLOPS = 2 * R * K * J + 2 * R * F * M

F32 = mybir.dt.float32
BF16 = mybir.dt.bfloat16
I32 = mybir.dt.int32
U32 = mybir.dt.uint32
U16 = mybir.dt.uint16
U8 = mybir.dt.uint8
FP8X4 = mybir.dt.float8_e4m3fn_x4
FP4X4 = mybir.dt.float4_e2m1fn_x4
ACT = mybir.ActivationFunctionType
ALU = mybir.AluOpType

P = 128
PACK = 4


def tile_attend_csoftleast_kernel(tc, tab_words, tab_scales, w1, temper, wo, dy, old, offs, offs2, offs3, offs4, out):
    nc = tc.nc
    with ExitStack() as ctx:
        keep = ctx.enter_context(tc.tile_pool(name="keep", bufs=1))
        psum = ctx.enter_context(tc.psum_pool(name="psum", bufs=1))

        slots = keep.tile([P, J // 16], U16)
        picks = [keep.tile([P, M // 16], U16, name="picks%d" % i) for i in range(3)]
        words = keep.tile([P, T], U16, align_bytes=64)
        plane = keep.tile([P, T], U8, align_bytes=64)
        w1_raw = keep.tile([P, PACK * R], F32)
        placed = [keep.tile([P, J], F32, name="placed%d" % i) for i in range(3)]
        ident = keep.tile([P, P], F32)

        plane32 = plane[:].bitcast(I32)
        nc.vector.memset(plane32, 0)
        temper_col = keep.tile([P, 1], F32)
        nc.sync.dma_start(slots[:], offs)
        nc.scalar.dma_start(out=w1_raw[:], in_=w1.rearrange("(p j) w -> p (j w)", j=PACK))
        nc.scalar.dma_start(out=temper_col[:], in_=temper)
        for tile, src in zip(picks, (offs2, offs3, offs4)):
            nc.sync.dma_start(tile[:], src)
        nc.sync.dma_start(out=words[:].bitcast(I32), in_=tab_words[0].bitcast(I32))
        scales32 = tab_scales[0].bitcast(I32)
        for r in range(4):
            nc.sync.dma_start(out=plane32[r:P:32, :], in_=scales32[r:16:4, :])

        zeros = keep.tile([P, P], F32, tag="after_zeros")
        nc.vector.memset(zeros[:], 0.0)
        nc.gpsimd.affine_select(out=ident[:], in_=zeros[:], compare_op=ALU.not_equal, fill=1.0, base=0,
                                pattern=[[-1, P]], channel_multiplier=1)
        for tile in placed:
            nc.vector.memset(tile[:], 0.0)

        later = keep.tile([P, PACK * (R + M) + J], F32, tag="after_zeros")
        wo_raw = later[:, : PACK * R]
        dy_raw = later[:, PACK * R : PACK * (R + M)]
        old_sb = later[:, PACK * (R + M) :]
        nc.sync.dma_start(out=wo_raw, in_=wo.rearrange("(p j) w -> p (j w)", j=PACK))
        nc.sync.dma_start(out=dy_raw, in_=dy.rearrange("(p j) w -> p (j w)", j=PACK))
        nc.sync.dma_start(out=old_sb, in_=old)

        def interleave(copy, name, raw, width):
            grouped = keep.tile([P, width, PACK], BF16, align_bytes=64, name=name + "_grouped", tag=name + "_grouped")
            copy(out=grouped[:].rearrange("p (c i) j -> p c j i", i=PACK), in_=raw.rearrange("p (j c i) -> p c j i", j=PACK, i=PACK))
            return grouped

        def quantize(name, grouped, width):
            codes = keep.tile([P, width], U32, align_bytes=64, name=name + "_codes")
            scales = keep.tile([P, width], U8, align_bytes=64, name=name + "_scales")
            nc.vector.quantize_mx(out=codes[:].bitcast(FP8X4), scales=scales[:], in_=grouped[:].rearrange("p w j -> p (w j)"))
            return codes, scales

        w1_grouped = interleave(nc.scalar.copy, "w1", w1_raw[:], R)

        wo_grouped = interleave(nc.scalar.copy, "wo", wo_raw, R)
        minus_temper = wo_raw[:, 0:1]
        nc.scalar.activation(out=minus_temper, in_=temper_col[:], func=ACT.Copy, scale=-1.0)

        HALF = J // 2
        got_words = [keep.tile([P, HALF], U16, align_bytes=64, name="got_words%d" % h) for h in range(2)]
        got_scales = [keep.tile([P, HALF], U8, align_bytes=64, name="got_scales%d" % h) for h in range(2)]
        lists = [slots[:, h * HALF // 16 : (h + 1) * HALF // 16] for h in range(2)]
        w1_codes, w1_scales = quantize("w1", w1_grouped, R)
        for h in range(2):
            nc.vector.tensor_copy(got_words[h][:], words[:].indirect(lists[h]))
        for h in range(2):
            nc.vector.tensor_copy(got_scales[h][:], plane[:].indirect(lists[h]))

        e1s = keep.tile([P, J], F32)
        for h, lo, hi, bank in ((0, 0, HALF, "half0"), (1, 0, P, "third"), (1, P, HALF, "half1")):
            a = psum.tile([P, hi - lo], F32, name="a_" + bank, tag=bank)
            nc.tensor.matmul_mx(out=a[:], lhsT=w1_codes[:].bitcast(FP8X4), lhsT_scale=w1_scales[:],
                                rhs=got_words[h][:, lo:hi].bitcast(FP4X4), rhs_scale=got_scales[h][:, lo:hi], start=True, stop=True)
            nc.scalar.activation(out=e1s[:, h * HALF + lo : h * HALF + hi], in_=a[:], func=ACT.Exp, scale=minus_temper)

        warm = keep.tile([P, 1], F32)
        nc.scalar.activation(out=warm[:], in_=a[:, 0:1], func=ACT.Abs_reciprocal_sqrt, scale=0.0, bias=1.0)

        PART = M // 2
        first, second = slice(0, PART), slice(PART, M)
        dy_grouped = interleave(nc.vector.tensor_copy, "dy", dy_raw, M)
        wo_codes, wo_scales = quantize("wo", wo_grouped, R)
        dy_codes, dy_scales = quantize("dy", dy_grouped, M)
        c0 = psum.tile([P, M], F32)
        nc.tensor.matmul_mx(out=c0[:], lhsT=wo_codes[:].bitcast(FP8X4), lhsT_scale=wo_scales[:],
                            rhs=dy_codes[:].bitcast(FP8X4), rhs_scale=dy_scales[:], start=True, stop=True)

        picked = keep.tile([P, 3 * M], F32, align_bytes=64, tag="dy_grouped")
        got = [picked[:, i * M : (i + 1) * M] for i in range(3)]
        products = keep.tile([P, 3 * M], F32)
        weighted = [products[:, i * M : (i + 1) * M] for i in range(3)]
        pair = (products[:, 2 * M : 2 * M + PART], products[:, M - PART // 2 : M + PART // 2])
        s = keep.tile([P, M], F32)
        root = keep.tile([P, M], F32)
        inv = keep.tile([P, M], F32)
        for i in range(3):
            nc.vector.tensor_copy(got[i], e1s[:].indirect(picks[i][:]))
        for h, cols in enumerate((first, second)):
            nc.vector.tensor_tensor(pair[h], got[0][:, cols], got[1][:, cols], ALU.add)
        for h, cols in enumerate((first, second)):
            nc.vector.tensor_tensor(s[:, cols], pair[h], got[2][:, cols], ALU.add)
            nc.scalar.activation(out=root[:, cols], in_=s[:, cols], func=ACT.Abs_reciprocal_sqrt)
        for cols in (first, second):
            nc.scalar.activation(out=inv[:, cols], in_=root[:, cols], func=ACT.Square)
        for i in range(3):
            nc.vector.tensor_tensor(weighted[i], c0[:], got[i], ALU.mult)
        for i in range(3):
            nc.vector.tensor_tensor(placed[i][:].indirect(picks[i][:]), weighted[i], inv[:], ALU.mult)

        turned = keep.tile([P, J], F32)
        back = [psum.tile([P, HALF], F32, name="back%d" % h, tag="half%d" % h) for h in range(2)]
        sums = [psum.tile([P, P], F32, name="sums%d" % b) for b in range(J // P)]
        terms = (old_sb, placed[0][:], placed[1][:])
        for n, term in enumerate(terms):
            for b in range(J // P):
                nc.tensor.matmul(out=sums[b][:], lhsT=term[:, b * P : (b + 1) * P], rhs=ident[:],
                                 start=(n == 0), stop=(n == len(terms) - 1), is_transpose=True)
        for b in range(J // P):
            nc.scalar.copy(out=turned[:, b * P : (b + 1) * P], in_=sums[b][:])
        for b in range(J // P):
            nc.tensor.transpose(back[b // 2][:, b % 2 * P : (b % 2 + 1) * P], turned[:, b * P : (b + 1) * P], ident[:])

        result = [keep.tile([P, HALF], F32, name="result%d" % h) for h in range(2)]
        for h, queue in enumerate((nc.sync, nc.scalar)):
            cols = slice(h * HALF, (h + 1) * HALF)
            nc.vector.tensor_tensor(result[h][:], back[h][:], placed[2][:, cols], ALU.add)
            queue.dma_start(out=out[:, cols], in_=result[h][:])
